import numpy as np
import ml_dtypes

BF16 = ml_dtypes.bfloat16


def bf(x):
    return np.asarray(x, np.float32).astype(BF16)


def f32(x):
    return np.asarray(x, np.float32)


def f64(x):
    return np.asarray(x).astype(np.float64)


def striped(idx):
    return np.tile(idx.reshape(-1, 16).T, (8, 1))


S, K, M, N, D, V = 256, 128, 512, 384, 4, 96


def setup_inputs():
    return {"table": bf(np.random.standard_normal((S, K))), "w": bf(np.random.standard_normal((K, M)) / np.sqrt(D * K)), "c": f32(0.2 + 0.8 * np.random.random_sample((1, V))), "offs": striped(np.random.permutation(np.tile(np.arange(S), 2))[:N])}


def reference(table, w, c, offs):
    idx = offs[:16].T.reshape(-1)
    x = f64(table)[idx].T
    y = f64(w).T @ sum(x[:, t * V : (t + 1) * V] for t in range(D))
    return y * f64(c)

@@ -1,0 +1,55 @@
+import concourse.mybir as mybir
+from concourse.masks import make_identity
+
+BF16, F32, U16 = mybir.dt.bfloat16, mybir.dt.float32, mybir.dt.uint16
+
+P = 128
+S, K, M = 256, 128, 512
+D, V = 4, 96
+N = D * V
+PIECE_COLS = V // 16
+
+FLOPS = 2 * K * M * V
+
+
+def tile_gather_matmul_kernel(tc, table, w, c, offs, out):
+    nc = tc.nc
+    with (
+        tc.tile_pool(name="held", bufs=1) as held,
+        tc.tile_pool(name="scaled", bufs=M // P) as scaled_pool,
+        tc.psum_pool(name="flip", bufs=S // P) as flip_pool,
+        tc.psum_pool(name="sums", bufs=M // P) as sums_pool,
+    ):
+        offsets = held.tile([P, N // 16], U16, name="offsets")
+        nc.sync.dma_start(offsets[:], offs)
+        rows = held.tile([P, S // P, K], BF16, name="rows")
+        nc.scalar.dma_start(rows[:], table.rearrange("(b p) k -> p b k", p=P))
+        weights = held.tile([K, M], BF16, name="weights")
+        nc.sync.dma_start(weights[:], w)
+        c_all = held.tile([P, V], F32, name="c_all")
+        nc.scalar.dma_start(c_all[:], c.rearrange("o v -> (o v)").partition_broadcast(P))
+
+        identity = held.tile([P, P], BF16, name="identity")
+        make_identity(nc, identity[:])
+
+        features = held.tile([K, S], BF16, name="features")
+        for b in range(S // P):
+            flipped = flip_pool.tile([K, P], BF16, name="flipped")
+            nc.tensor.transpose(flipped[:], rows[:, b, :], identity[:])
+            nc.vector.tensor_copy(features[:, b * P : (b + 1) * P], flipped[:])
+
+        for a in range(M // P):
+            sums = sums_pool.tile([P, V], F32, name="sums")
+            for t in range(D):
+                piece = offsets[:, t * PIECE_COLS : (t + 1) * PIECE_COLS]
+                nc.tensor.matmul(
+                    sums[:],
+                    weights[:, a * P : (a + 1) * P],
+                    features[:].indirect(piece),
+                    start=(t == 0),
+                    stop=(t == D - 1),
+                )
+            scaled = scaled_pool.tile([P, V], F32, name="scaled")
+            nc.vector.tensor_tensor(scaled[:], sums[:], c_all[:], mybir.AluOpType.mult)
+            queue = nc.sync if a % 2 == 0 else nc.scalar
+            queue.dma_start(out[a * P : (a + 1) * P, :], scaled[:])

@@ -11,6 +11,8 @@ PIECE_COLS = V // 16
 
 FLOPS = 2 * K * M * V
 
+WARM_MATMULS, WARM_COLS = 16, 128
+
 
 def tile_gather_matmul_kernel(tc, table, w, c, offs, out):
     nc = tc.nc
@@ -19,6 +21,7 @@ def tile_gather_matmul_kernel(tc, table, w, c, offs, out):
         tc.tile_pool(name="scaled", bufs=M // P) as scaled_pool,
         tc.psum_pool(name="flip", bufs=S // P) as flip_pool,
         tc.psum_pool(name="sums", bufs=M // P) as sums_pool,
+        tc.psum_pool(name="idle", bufs=1) as idle_pool,
     ):
         offsets = held.tile([P, N // 16], U16, name="offsets")
         nc.sync.dma_start(offsets[:], offs)
@@ -28,6 +31,12 @@ def tile_gather_matmul_kernel(tc, table, w, c, offs, out):
         nc.sync.dma_start(weights[:], w)
         c_all = held.tile([P, V], F32, name="c_all")
         nc.scalar.dma_start(c_all[:], c.rearrange("o v -> (o v)").partition_broadcast(P))
+
+        zeros = held.tile([P, WARM_COLS], BF16, name="zeros")
+        nc.gpsimd.memset(zeros[:], 0.0)
+        unread = idle_pool.tile([P, WARM_COLS], F32, name="unread")
+        for i in range(WARM_MATMULS):
+            nc.tensor.matmul(unread[:], zeros[:, 0:P], zeros[:], start=True, stop=True)
 
         identity = held.tile([P, P], BF16, name="identity")
         make_identity(nc, identity[:])

@@ -11,7 +11,7 @@ PIECE_COLS = V // 16
 
 FLOPS = 2 * K * M * V
 
-WARM_MATMULS, WARM_COLS = 16, 128
+BUSY_DURING_LOADS, BUSY_DURING_COPIES = 8, 4
 
 
 def tile_gather_matmul_kernel(tc, table, w, c, offs, out):
@@ -32,11 +32,15 @@ def tile_gather_matmul_kernel(tc, table, w, c, offs, out):
         c_all = held.tile([P, V], F32, name="c_all")
         nc.scalar.dma_start(c_all[:], c.rearrange("o v -> (o v)").partition_broadcast(P))
 
-        zeros = held.tile([P, WARM_COLS], BF16, name="zeros")
-        nc.gpsimd.memset(zeros[:], 0.0)
-        unread = idle_pool.tile([P, WARM_COLS], F32, name="unread")
-        for i in range(WARM_MATMULS):
-            nc.tensor.matmul(unread[:], zeros[:, 0:P], zeros[:], start=True, stop=True)
+        zeros = held.tile([P, P], BF16, name="zeros")
+        nc.vector.memset(zeros[:], 0.0)
+        unread = idle_pool.tile([P, P], F32, name="unread")
+
+        def keep_tensor_engine_busy(matmuls):
+            for i in range(matmuls):
+                nc.tensor.matmul(unread[:], zeros[:], zeros[:], start=True, stop=True)
+
+        keep_tensor_engine_busy(BUSY_DURING_LOADS)
 
         identity = held.tile([P, P], BF16, name="identity")
         make_identity(nc, identity[:])
@@ -46,6 +50,8 @@ def tile_gather_matmul_kernel(tc, table, w, c, offs, out):
             flipped = flip_pool.tile([K, P], BF16, name="flipped")
             nc.tensor.transpose(flipped[:], rows[:, b, :], identity[:])
             nc.vector.tensor_copy(features[:, b * P : (b + 1) * P], flipped[:])
+
+        keep_tensor_engine_busy(BUSY_DURING_COPIES)
 
         for a in range(M // P):
             sums = sums_pool.tile([P, V], F32, name="sums")

@@ -28,7 +28,7 @@ def tile_gather_matmul_kernel(tc, table, w, c, offs, out):
         rows = held.tile([P, S // P, K], BF16, name="rows")
         nc.scalar.dma_start(rows[:], table.rearrange("(b p) k -> p b k", p=P))
         weights = held.tile([K, M], BF16, name="weights")
-        nc.sync.dma_start(weights[:], w)
+        nc.scalar.dma_start(weights[:], w)
         c_all = held.tile([P, V], F32, name="c_all")
         nc.scalar.dma_start(c_all[:], c.rearrange("o v -> (o v)").partition_broadcast(P))
 

@@ -23,14 +23,14 @@ def tile_gather_matmul_kernel(tc, table, w, c, offs, out):
         tc.psum_pool(name="sums", bufs=M // P) as sums_pool,
         tc.psum_pool(name="idle", bufs=1) as idle_pool,
     ):
+        rows = held.tile([P, S // P, K], BF16, name="rows")
+        nc.sync.dma_start(rows[:], table.rearrange("(b p) k -> p b k", p=P))
         offsets = held.tile([P, N // 16], U16, name="offsets")
         nc.sync.dma_start(offsets[:], offs)
-        rows = held.tile([P, S // P, K], BF16, name="rows")
-        nc.scalar.dma_start(rows[:], table.rearrange("(b p) k -> p b k", p=P))
         weights = held.tile([K, M], BF16, name="weights")
-        nc.scalar.dma_start(weights[:], w)
+        nc.sync.dma_start(weights[:], w)
         c_all = held.tile([P, V], F32, name="c_all")
-        nc.scalar.dma_start(c_all[:], c.rearrange("o v -> (o v)").partition_broadcast(P))
+        nc.sync.dma_start(c_all[:], c.rearrange("o v -> (o v)").partition_broadcast(P))
 
         zeros = held.tile([P, P], BF16, name="zeros")
         nc.vector.memset(zeros[:], 0.0)

@@ -11,8 +11,6 @@ PIECE_COLS = V // 16
 
 FLOPS = 2 * K * M * V
 
-BUSY_DURING_LOADS, BUSY_DURING_COPIES = 8, 4
-
 
 def tile_gather_matmul_kernel(tc, table, w, c, offs, out):
     nc = tc.nc
@@ -21,7 +19,6 @@ def tile_gather_matmul_kernel(tc, table, w, c, offs, out):
         tc.tile_pool(name="scaled", bufs=M // P) as scaled_pool,
         tc.psum_pool(name="flip", bufs=S // P) as flip_pool,
         tc.psum_pool(name="sums", bufs=M // P) as sums_pool,
-        tc.psum_pool(name="idle", bufs=1) as idle_pool,
     ):
         rows = held.tile([P, S // P, K], BF16, name="rows")
         nc.sync.dma_start(rows[:], table.rearrange("(b p) k -> p b k", p=P))
@@ -32,16 +29,6 @@ def tile_gather_matmul_kernel(tc, table, w, c, offs, out):
         c_all = held.tile([P, V], F32, name="c_all")
         nc.sync.dma_start(c_all[:], c.rearrange("o v -> (o v)").partition_broadcast(P))
 
-        zeros = held.tile([P, P], BF16, name="zeros")
-        nc.vector.memset(zeros[:], 0.0)
-        unread = idle_pool.tile([P, P], F32, name="unread")
-
-        def keep_tensor_engine_busy(matmuls):
-            for i in range(matmuls):
-                nc.tensor.matmul(unread[:], zeros[:], zeros[:], start=True, stop=True)
-
-        keep_tensor_engine_busy(BUSY_DURING_LOADS)
-
         identity = held.tile([P, P], BF16, name="identity")
         make_identity(nc, identity[:])
 
@@ -50,8 +37,6 @@ def tile_gather_matmul_kernel(tc, table, w, c, offs, out):
             flipped = flip_pool.tile([K, P], BF16, name="flipped")
             nc.tensor.transpose(flipped[:], rows[:, b, :], identity[:])
             nc.vector.tensor_copy(features[:, b * P : (b + 1) * P], flipped[:])
-
-        keep_tensor_engine_busy(BUSY_DURING_COPIES)
 
         for a in range(M // P):
             sums = sums_pool.tile([P, V], F32, name="sums")

@@ -38,18 +38,21 @@ def tile_gather_matmul_kernel(tc, table, w, c, offs, out):
             nc.tensor.transpose(flipped[:], rows[:, b, :], identity[:])
             nc.vector.tensor_copy(features[:, b * P : (b + 1) * P], flipped[:])
 
-        for a in range(M // P):
-            sums = sums_pool.tile([P, V], F32, name="sums")
+        for pair in range(M // P // 2):
+            blocks = (2 * pair, 2 * pair + 1)
+            sums = {a: sums_pool.tile([P, V], F32, name="sums") for a in blocks}
             for t in range(D):
                 piece = offsets[:, t * PIECE_COLS : (t + 1) * PIECE_COLS]
-                nc.tensor.matmul(
-                    sums[:],
-                    weights[:, a * P : (a + 1) * P],
-                    features[:].indirect(piece),
-                    start=(t == 0),
-                    stop=(t == D - 1),
-                )
-            scaled = scaled_pool.tile([P, V], F32, name="scaled")
-            nc.vector.tensor_tensor(scaled[:], sums[:], c_all[:], mybir.AluOpType.mult)
-            queue = nc.sync if a % 2 == 0 else nc.scalar
-            queue.dma_start(out[a * P : (a + 1) * P, :], scaled[:])
+                for a in blocks:
+                    nc.tensor.matmul(
+                        sums[a][:],
+                        weights[:, a * P : (a + 1) * P],
+                        features[:].indirect(piece),
+                        start=(t == 0),
+                        stop=(t == D - 1),
+                    )
+            for a in blocks:
+                scaled = scaled_pool.tile([P, V], F32, name="scaled")
+                nc.vector.tensor_tensor(scaled[:], sums[a][:], c_all[:], mybir.AluOpType.mult)
+                queue = nc.sync if a % 2 == 0 else nc.scalar
+                queue.dma_start(out[a * P : (a + 1) * P, :], scaled[:])

import concourse.mybir as mybir
from concourse.masks import make_identity

BF16, F32, U16 = mybir.dt.bfloat16, mybir.dt.float32, mybir.dt.uint16

P = 128
S, K, M = 256, 128, 512
D, V = 4, 96
N = D * V
PIECE_COLS = V // 16

FLOPS = 2 * K * M * V


def tile_gather_matmul_kernel(tc, table, w, c, offs, out):
    nc = tc.nc
    with (
        tc.tile_pool(name="held", bufs=1) as held,
        tc.tile_pool(name="scaled", bufs=M // P) as scaled_pool,
        tc.psum_pool(name="flip", bufs=S // P) as flip_pool,
        tc.psum_pool(name="sums", bufs=M // P) as sums_pool,
    ):
        rows = held.tile([P, S // P, K], BF16, name="rows")
        nc.sync.dma_start(rows[:], table.rearrange("(b p) k -> p b k", p=P))
        offsets = held.tile([P, N // 16], U16, name="offsets")
        nc.sync.dma_start(offsets[:], offs)
        weights = held.tile([K, M], BF16, name="weights")
        nc.sync.dma_start(weights[:], w)
        c_all = held.tile([P, V], F32, name="c_all")
        nc.sync.dma_start(c_all[:], c.rearrange("o v -> (o v)").partition_broadcast(P))

        identity = held.tile([P, P], BF16, name="identity")
        make_identity(nc, identity[:])

        features = held.tile([K, S], BF16, name="features")
        for b in range(S // P):
            flipped = flip_pool.tile([K, P], BF16, name="flipped")
            nc.tensor.transpose(flipped[:], rows[:, b, :], identity[:])
            nc.vector.tensor_copy(features[:, b * P : (b + 1) * P], flipped[:])

        for pair in range(M // P // 2):
            blocks = (2 * pair, 2 * pair + 1)
            sums = {a: sums_pool.tile([P, V], F32, name="sums") for a in blocks}
            for t in range(D):
                piece = offsets[:, t * PIECE_COLS : (t + 1) * PIECE_COLS]
                for a in blocks:
                    nc.tensor.matmul(
                        sums[a][:],
                        weights[:, a * P : (a + 1) * P],
                        features[:].indirect(piece),
                        start=(t == 0),
                        stop=(t == D - 1),
                    )
            for a in blocks:
                scaled = scaled_pool.tile([P, V], F32, name="scaled")
                nc.vector.tensor_tensor(scaled[:], sums[a][:], c_all[:], mybir.AluOpType.mult)
                queue = nc.sync if a % 2 == 0 else nc.scalar
                queue.dma_start(out[a * P : (a + 1) * P, :], scaled[:])
